import numpy as np
import ml_dtypes


def mxq(x, axis, fmt="e4m3"):
    dtype, down = {"e4m3": (ml_dtypes.float8_e4m3fn, 7), "e5m2": (ml_dtypes.float8_e5m2, 14)}[fmt]
    v = np.moveaxis(np.asarray(x, np.float32).astype(ml_dtypes.bfloat16).astype(np.float64), axis, -1)
    blocks = v.reshape(v.shape[:-1] + (-1, 32))
    amax = np.abs(blocks).max(-1, keepdims=True)
    byte = np.maximum(np.where(amax > 0, np.frexp(amax)[1] - 1 + 127, 0) - down, 1)
    scale = np.exp2(byte - 127.0)
    codes = (blocks / scale).astype(np.float32).astype(dtype).astype(np.float64)
    return np.moveaxis((codes * scale).reshape(v.shape), -1, axis)


WIDE = False


def mx_kscale(k):
    if not WIDE:
        return np.ones(k)
    levels = np.array([10, -10, 5, -5, 0])
    if k % 512:
        return np.exp2(np.random.permutation(np.resize(levels, k // 32))).repeat(32)
    a = np.empty((k // 512, 16))
    for p in range(k // 512):
        a[p, :8] = np.random.permutation(np.resize(levels, 8))
        for g in range(8):
            far = levels[np.abs(levels - a[p, g]) >= 10]
            a[p, g + 8] = far[np.random.randint(len(far))]
    return np.exp2(a.ravel()).repeat(32)


def f64(x):
    return np.asarray(x).astype(np.float64)


def striped(idx):
    return np.tile(idx.reshape(-1, 16).T, (8, 1)).astype(np.uint16)


def unstriped(offs):
    return offs[:16].T.reshape(-1).astype(np.int64)


def striped8(idx):
    return np.concatenate([x.reshape(-1, 16).T for x in idx]).astype(np.uint16)


def runs(offs, k):
    lists = np.stack([offs[16 * r : 16 * r + 16].T.reshape(-1) for r in range(8)]).astype(np.int64)
    return lists[np.arange(k) % 512 // 64]


def pack_weight(w):
    k, n = w.shape
    w = f64(np.asarray(w, np.float32).astype(ml_dtypes.bfloat16)).reshape(k // 32, 32, n)
    amax = np.abs(w).max(1)
    byte = np.clip(np.where(amax > 0, np.frexp(amax)[1] - 1 + 127 - 7, 1), 1, 254)
    scaled = (w * np.exp2(127.0 - byte)[:, None, :]).reshape(k, n).astype(np.float32)
    words = np.ascontiguousarray(scaled.reshape(k // 512, 128, 4, n).transpose(0, 1, 3, 2)).astype(ml_dtypes.float8_e4m3fn).view(np.uint8)
    return words, np.ascontiguousarray(byte.astype(np.uint8).reshape(k // 512, 16, n))


def unpack_weight(words, scales):
    g, p, n, _ = words.shape
    vals = np.ascontiguousarray(words).view(ml_dtypes.float8_e4m3fn).astype(np.float64) * np.repeat(np.exp2(scales.astype(np.float64) - 127.0), 8, axis=1)[..., None]
    return vals.transpose(0, 1, 3, 2).reshape(g * 512, n)


K, T, S, H, C = 512, 2048, 512, 512, 512


def setup_inputs():
    n = np.random.standard_normal
    s = mx_kscale(K)[:, None]
    packed_xT = pack_weight(n((K, T)) * s)
    return {
        "x_words": packed_xT[0],
        "x_scales": packed_xT[1],
        "w1": (n((K, H)) / np.sqrt(K) / s).astype(np.float32),
        "gs": (np.random.uniform(0.5, 1.5, (K, 1)) / s).astype(np.float32),
        "offs": striped(np.random.permutation(T)[:S]),
        "n1": striped8(np.stack([np.random.permutation(S) for _ in range(8)])),
        "n2": striped8(np.stack([np.random.permutation(S) for _ in range(8)])),
        "n3": striped8(np.stack([np.random.permutation(S) for _ in range(8)])),
        "n4": striped8(np.stack([np.random.permutation(S) for _ in range(8)])),
        "cand": striped(np.random.permutation(T)[:C]),
        "n5": striped8(np.stack([np.random.permutation(S) for _ in range(8)])),
        "n6": striped8(np.stack([np.random.permutation(S) for _ in range(8)])),
    }


def reference(x_words, x_scales, w1, gs, offs, n1, n2, n3, n4, cand, n5, n6):
    x_cand = unpack_weight(x_words, x_scales)[:, unstriped(cand)]
    xq = unpack_weight(x_words, x_scales)[:, unstriped(offs)]
    y = mxq(f64(w1), 0, "e4m3").T @ xq
    z = f64(gs) * (0.75 * ((y[np.arange(H)[:, None], runs(n1, H)]) * (y[np.arange(H)[:, None], runs(n2, H)]) - ((y[np.arange(H)[:, None], runs(n3, H)]) * (y[np.arange(H)[:, None], runs(n4, H)]))))
    s = 0.0625 * ((x_cand.T @ mxq(z, 0, "e4m3")))
    return np.minimum(np.maximum(s, s[np.arange(C)[:, None], runs(n5, C)]), s[np.arange(C)[:, None], runs(n6, C)])

@@ -1,0 +1,207 @@
+from contextlib import ExitStack
+
+import concourse.mybir as mybir
+
+K, T, S, H, C = 512, 2048, 512, 512, 512
+FLOPS = 2 * K * H * S + 2 * K * C * S
+
+F32 = mybir.dt.float32
+BF16 = mybir.dt.bfloat16
+I32 = mybir.dt.int32
+U32 = mybir.dt.uint32
+U16 = mybir.dt.uint16
+U8 = mybir.dt.uint8
+FP8X4 = mybir.dt.float8_e4m3fn_x4
+ALU = mybir.AluOpType
+COPY = mybir.ActivationFunctionType.Copy
+
+P = 128
+PACK = 4
+WINDOW = 2 * S
+Z_PIECES = ((0, 256), (256, 384), (384, 512))
+
+
+def tile_picked_canddetminmx_none_p_kernel(
+    tc, x_words, x_scales, w1, gs, offs, n1, n2, n3, n4, cand, n5, n6, out
+):
+    nc = tc.nc
+    with ExitStack() as ctx:
+        keep = ctx.enter_context(tc.tile_pool(name="keep", bufs=1))
+        ring = ctx.enter_context(tc.tile_pool(name="ring", bufs=2))
+        psum = ctx.enter_context(tc.psum_pool(name="psum", bufs=1))
+
+        def load_list(name, source):
+            tile = keep.tile([P, S // 16], U16, name=name)
+            nc.sync.dma_start(tile[:], source)
+            return tile
+
+        table_bytes = keep.tile([P, T], U8, name="table_bytes", align_bytes=64)
+        nc.vector.memset(table_bytes[:].bitcast(I32), 0)
+        for q in range(4):
+            nc.scalar.dma_start(
+                table_bytes[32 * q : 32 * q + 4, :].bitcast(I32),
+                x_scales[0, 4 * q : 4 * q + 4, :].bitcast(I32),
+            )
+        offs_t = load_list("offs_t", offs)
+        cand_t = load_list("cand_t", cand)
+        table_words = keep.tile([P, T], I32, name="table_words", align_bytes=64)
+        nc.sync.dma_start(table_words[:], x_words[0].rearrange("p n r -> p (n r)").bitcast(I32))
+        w_rows = w1.rearrange("(p j) c -> p j c", j=PACK)
+        w_raw = []
+        for h in range(2):
+            half = keep.tile([P, PACK, H // 2], F32, name=f"w_raw{h}")
+            nc.sync.dma_start(half[:], w_rows[:, :, h * (H // 2) : (h + 1) * (H // 2)])
+            w_raw.append(half)
+        n1_t = load_list("n1_t", n1)
+        n3_t = load_list("n3_t", n3)
+        gs_raw = keep.tile([P, PACK], F32, name="gs_raw")
+        nc.sync.dma_start(gs_raw[:], gs.rearrange("(p t) o -> p (t o)", t=PACK))
+        n2_t = load_list("n2_t", n2)
+        n4_t = load_list("n4_t", n4)
+        n5_t = load_list("n5_t", n5)
+        n6_t = load_list("n6_t", n6)
+
+        windows = []
+        for w in range(4):
+            window = keep.tile([P, WINDOW], F32, name=f"window{w}")
+            nc.vector.memset(window[:, S:], 0.0)
+            windows.append(window)
+
+        def gather_packed(name, offsets):
+            scale_bytes = keep.tile([P, S], U8, name=name + "_bytes", align_bytes=64)
+            nc.vector.tensor_copy(scale_bytes[:], table_bytes[:].indirect(offsets[:]))
+            return scale_bytes
+
+        def gather_words(name, offsets):
+            words = keep.tile([P, S], U32, name=name + "_words", align_bytes=64)
+            nc.vector.tensor_copy(words[:], table_words[:].bitcast(U32).indirect(offsets[:]))
+            return words
+
+        xq_bytes = gather_packed("xq", offs_t)
+        xc_bytes = gather_packed("xc", cand_t)
+        xq_words = gather_words("xq", offs_t)
+        xc_words = gather_words("xc", cand_t)
+
+        dealt_words = keep.tile([P, C], U32, name="dealt_words", align_bytes=64)
+        dealt_bytes = keep.tile([P, C], U8, name="dealt_bytes", align_bytes=64)
+        nc.vector.tensor_copy(
+            dealt_bytes[:].rearrange("p (u m) -> p u m", u=PACK),
+            xc_bytes[:].rearrange("p (m u) -> p u m", u=PACK),
+        )
+        nc.vector.tensor_copy(
+            dealt_words[:].rearrange("p (u c i) -> p c u i", u=PACK, i=4),
+            xc_words[:].rearrange("p (c i u) -> p c u i", u=PACK, i=4),
+        )
+
+        gs_scaled = keep.tile([P, PACK], F32, name="gs_scaled")
+        left = keep.tile([P, PACK, S], F32, name="left")
+        right = keep.tile([P, PACK, S], F32, name="right")
+
+        def project(t):
+            w_bf = keep.tile([P, P, PACK], BF16, name=f"w_bf{t}", align_bytes=64)
+            for h in range(2):
+                nc.scalar.copy(
+                    w_bf[:, 64 * h : 64 * (h + 1), :],
+                    w_raw[h][:].rearrange("p j (m t) -> p t m j", t=PACK)[:, t],
+                )
+            w_words = keep.tile([P, P], U32, name=f"w_words{t}", align_bytes=64)
+            w_bytes = keep.tile([P, P], U8, name=f"w_bytes{t}", align_bytes=64)
+            nc.vector.quantize_mx(
+                out=w_words[:].bitcast(FP8X4),
+                scales=w_bytes[:],
+                in_=w_bf[:].rearrange("p m j -> p (m j)"),
+            )
+            y_bank = psum.tile([P, S], F32, name=f"y_bank{t}")
+            nc.tensor.matmul_mx(
+                out=y_bank[:],
+                lhsT=w_words[:].bitcast(FP8X4),
+                lhsT_scale=w_bytes[:],
+                rhs=xq_words[:].bitcast(FP8X4),
+                rhs_scale=xq_bytes[:],
+                start=True,
+                stop=True,
+            )
+            return y_bank
+
+        def empty_y(t, y_bank):
+            y, y_scaled = windows[2 * (t % 2)], windows[2 * (t % 2) + 1]
+            nc.scalar.copy(y[:, :S], y_bank[:])
+            if t == 0:
+                nc.scalar.activation(gs_scaled[:], gs_raw[:], COPY, scale=0.75)
+            nc.scalar.activation(y_scaled[:, :S], y_bank[:], COPY, scale=gs_scaled[:, t : t + 1])
+
+        def look_up_y(t):
+            y, y_scaled = windows[2 * (t % 2)], windows[2 * (t % 2) + 1]
+            y1 = ring.tile([P, S], F32, name="y1")
+            y3 = ring.tile([P, S], F32, name="y3")
+            nc.vector.tensor_copy(y1[:], y[:].indirect(n1_t[:]))
+            nc.vector.tensor_copy(y3[:], y[:].indirect(n3_t[:]))
+            nc.vector.tensor_tensor(left[:, t, :], y_scaled[:].indirect(n2_t[:]), y1[:], ALU.mult)
+            nc.vector.tensor_tensor(right[:, t, :], y_scaled[:].indirect(n4_t[:]), y3[:], ALU.mult)
+
+        empty_y(0, project(0))
+        for t in range(PACK):
+            if t + 1 < PACK:
+                empty_y(t + 1, project(t + 1))
+            look_up_y(t)
+
+        s_banks = [psum.tile([P, S], F32, name=f"s_bank{u}") for u in range(PACK)]
+        z_words = keep.tile([P, S], U32, name="z_words", align_bytes=64)
+        z_bytes = keep.tile([P, S], U8, name="z_bytes", align_bytes=64)
+
+        def subtract(lo, hi):
+            z_bf = keep.tile([P, (hi - lo) * PACK], BF16, name=f"z_bf{lo}", align_bytes=64)
+            nc.vector.tensor_tensor(
+                z_bf[:].rearrange("p (c i t) -> p c t i", i=2, t=PACK),
+                left[:, :, lo:hi].rearrange("p t (c i) -> p c t i", i=2),
+                right[:, :, lo:hi].rearrange("p t (c i) -> p c t i", i=2),
+                ALU.subtract,
+            )
+            return z_bf
+
+        def score(lo, hi, z_bf):
+            nc.vector.quantize_mx(
+                out=z_words[:, lo:hi].bitcast(FP8X4), scales=z_bytes[:, lo:hi], in_=z_bf[:]
+            )
+            for u in range(PACK):
+                nc.tensor.matmul_mx(
+                    out=s_banks[u][:, lo:hi],
+                    lhsT=dealt_words[:, P * u : P * (u + 1)].bitcast(FP8X4),
+                    lhsT_scale=dealt_bytes[:, P * u : P * (u + 1)],
+                    rhs=z_words[:, lo:hi].bitcast(FP8X4),
+                    rhs_scale=z_bytes[:, lo:hi],
+                    start=True,
+                    stop=True,
+                )
+            nc.scalar.activation(windows[0][:, lo:hi], s_banks[0][:, lo:hi], COPY, scale=0.0625)
+
+        pending = None
+        for lo, hi in Z_PIECES:
+            z_bf = subtract(lo, hi)
+            if pending is not None:
+                score(*pending)
+            pending = (lo, hi, z_bf)
+        score(*pending)
+        for u in range(1, PACK):
+            nc.scalar.activation(windows[u][:, :S], s_banks[u][:], COPY, scale=0.0625)
+
+        out_rows = out.rearrange("(p u) j -> p u j", u=PACK)
+
+        def finish(u, larger, s6):
+            result = keep.tile([P, S], F32, name=f"result{u}")
+            nc.vector.tensor_tensor(result[:], larger[:], s6[:], ALU.min)
+            nc.sync.dma_start(out_rows[:, u, :], result[:])
+
+        pending = None
+        for u in range(PACK):
+            s = windows[u]
+            s5 = ring.tile([P, S], F32, name="s5")
+            s6 = ring.tile([P, S], F32, name="s6")
+            larger = ring.tile([P, S], F32, name="larger")
+            nc.vector.tensor_copy(s5[:], s[:].indirect(n5_t[:]))
+            if pending is not None:
+                finish(*pending)
+            nc.vector.tensor_copy(s6[:], s[:].indirect(n6_t[:]))
+            nc.vector.tensor_tensor(larger[:], s5[:], s[:, :S], ALU.max)
+            pending = (u, larger, s6)
+        finish(*pending)

@@ -36,26 +36,25 @@ def tile_picked_canddetminmx_none_p_kernel(
             return tile
 
         table_bytes = keep.tile([P, T], U8, name="table_bytes", align_bytes=64)
-        nc.vector.memset(table_bytes[:].bitcast(I32), 0)
+        nc.vector.memset(table_bytes[:, : T // 2].bitcast(I32), 0)
+        nc.gpsimd.memset(table_bytes[:, T // 2 :].bitcast(I32), 0)
+        offs_t = load_list("offs_t", offs)
+        w_rows = w1.rearrange("(p j) c -> p j c", j=PACK)
+        w_raw = [keep.tile([P, PACK, H // 2], F32, name=f"w_raw{h}") for h in range(2)]
+        nc.sync.dma_start(w_raw[0][:], w_rows[:, :, : H // 2])
+        cand_t = load_list("cand_t", cand)
         for q in range(4):
-            nc.scalar.dma_start(
+            nc.sync.dma_start(
                 table_bytes[32 * q : 32 * q + 4, :].bitcast(I32),
                 x_scales[0, 4 * q : 4 * q + 4, :].bitcast(I32),
             )
-        offs_t = load_list("offs_t", offs)
-        cand_t = load_list("cand_t", cand)
+        nc.sync.dma_start(w_raw[1][:], w_rows[:, :, H // 2 :])
         table_words = keep.tile([P, T], I32, name="table_words", align_bytes=64)
         nc.sync.dma_start(table_words[:], x_words[0].rearrange("p n r -> p (n r)").bitcast(I32))
-        w_rows = w1.rearrange("(p j) c -> p j c", j=PACK)
-        w_raw = []
-        for h in range(2):
-            half = keep.tile([P, PACK, H // 2], F32, name=f"w_raw{h}")
-            nc.sync.dma_start(half[:], w_rows[:, :, h * (H // 2) : (h + 1) * (H // 2)])
-            w_raw.append(half)
         n1_t = load_list("n1_t", n1)
-        n3_t = load_list("n3_t", n3)
         gs_raw = keep.tile([P, PACK], F32, name="gs_raw")
         nc.sync.dma_start(gs_raw[:], gs.rearrange("(p t) o -> p (t o)", t=PACK))
+        n3_t = load_list("n3_t", n3)
         n2_t = load_list("n2_t", n2)
         n4_t = load_list("n4_t", n4)
         n5_t = load_list("n5_t", n5)
@@ -64,53 +63,59 @@ def tile_picked_canddetminmx_none_p_kernel(
         windows = []
         for w in range(4):
             window = keep.tile([P, WINDOW], F32, name=f"window{w}")
-            nc.vector.memset(window[:, S:], 0.0)
+            nc.gpsimd.memset(window[:, S:], 0.0)
             windows.append(window)
 
-        def gather_packed(name, offsets):
-            scale_bytes = keep.tile([P, S], U8, name=name + "_bytes", align_bytes=64)
+        def gather_bytes(name, offsets):
+            scale_bytes = keep.tile([P, S], U8, name=name, align_bytes=64)
             nc.vector.tensor_copy(scale_bytes[:], table_bytes[:].indirect(offsets[:]))
             return scale_bytes
 
         def gather_words(name, offsets):
-            words = keep.tile([P, S], U32, name=name + "_words", align_bytes=64)
+            words = keep.tile([P, S], U32, name=name, align_bytes=64)
             nc.vector.tensor_copy(words[:], table_words[:].bitcast(U32).indirect(offsets[:]))
             return words
 
-        xq_bytes = gather_packed("xq", offs_t)
-        xc_bytes = gather_packed("xc", cand_t)
-        xq_words = gather_words("xq", offs_t)
-        xc_words = gather_words("xc", cand_t)
+        def quantise_w(t):
+            w_bf = ring.tile([P, P, PACK], BF16, name="w_bf", align_bytes=64)
+            for h in range(2):
+                nc.scalar.copy(
+                    w_bf[:, 64 * h : 64 * (h + 1), :],
+                    w_raw[h][:].rearrange("p j (m t) -> p t m j", t=PACK)[:, t],
+                )
+            w_words = ring.tile([P, P], U32, name="w_words", align_bytes=64)
+            w_bytes = ring.tile([P, P], U8, name="w_bytes", align_bytes=64)
+            nc.vector.quantize_mx(
+                out=w_words[:].bitcast(FP8X4),
+                scales=w_bytes[:],
+                in_=w_bf[:].rearrange("p m j -> p (m j)"),
+            )
+            return w_words, w_bytes
 
-        dealt_words = keep.tile([P, C], U32, name="dealt_words", align_bytes=64)
-        dealt_bytes = keep.tile([P, C], U8, name="dealt_bytes", align_bytes=64)
-        nc.vector.tensor_copy(
-            dealt_bytes[:].rearrange("p (u m) -> p u m", u=PACK),
-            xc_bytes[:].rearrange("p (m u) -> p u m", u=PACK),
-        )
-        nc.vector.tensor_copy(
-            dealt_words[:].rearrange("p (u c i) -> p c u i", u=PACK, i=4),
-            xc_words[:].rearrange("p (c i u) -> p c u i", u=PACK, i=4),
-        )
+        def deal(name, first, count):
+            words = keep.tile([P, count, P], U32, name=name + "_words", align_bytes=64)
+            scale_bytes = keep.tile([P, count, P], U8, name=name + "_bytes", align_bytes=64)
+            nc.vector.tensor_copy(
+                scale_bytes[:], xc_bytes[:].rearrange("p (m u) -> p u m", u=PACK)[:, first : first + count, :]
+            )
+            nc.vector.tensor_copy(
+                words[:].rearrange("p u (c i) -> p c u i", i=4),
+                xc_words[:].rearrange("p (c i u) -> p c u i", u=PACK, i=4)[:, :, first : first + count, :],
+            )
+            return [(words[:, u, :], scale_bytes[:, u, :]) for u in range(count)]
+
+        xq_bytes = gather_bytes("xq_bytes", offs_t)
+        xc_bytes = gather_bytes("xc_bytes", cand_t)
+        w_packed = [quantise_w(0), quantise_w(1)]
+        xq_words = gather_words("xq_words", offs_t)
+        xc_words = gather_words("xc_words", cand_t)
 
         gs_scaled = keep.tile([P, PACK], F32, name="gs_scaled")
         left = keep.tile([P, PACK, S], F32, name="left")
         right = keep.tile([P, PACK, S], F32, name="right")
 
         def project(t):
-            w_bf = keep.tile([P, P, PACK], BF16, name=f"w_bf{t}", align_bytes=64)
-            for h in range(2):
-                nc.scalar.copy(
-                    w_bf[:, 64 * h : 64 * (h + 1), :],
-                    w_raw[h][:].rearrange("p j (m t) -> p t m j", t=PACK)[:, t],
-                )
-            w_words = keep.tile([P, P], U32, name=f"w_words{t}", align_bytes=64)
-            w_bytes = keep.tile([P, P], U8, name=f"w_bytes{t}", align_bytes=64)
-            nc.vector.quantize_mx(
-                out=w_words[:].bitcast(FP8X4),
-                scales=w_bytes[:],
-                in_=w_bf[:].rearrange("p m j -> p (m j)"),
-            )
+            w_words, w_bytes = w_packed[t]
             y_bank = psum.tile([P, S], F32, name=f"y_bank{t}")
             nc.tensor.matmul_mx(
                 out=y_bank[:],
@@ -121,9 +126,6 @@ def tile_picked_canddetminmx_none_p_kernel(
                 start=True,
                 stop=True,
             )
-            return y_bank
-
-        def empty_y(t, y_bank):
             y, y_scaled = windows[2 * (t % 2)], windows[2 * (t % 2) + 1]
             nc.scalar.copy(y[:, :S], y_bank[:])
             if t == 0:
@@ -136,13 +138,15 @@ def tile_picked_canddetminmx_none_p_kernel(
             y3 = ring.tile([P, S], F32, name="y3")
             nc.vector.tensor_copy(y1[:], y[:].indirect(n1_t[:]))
             nc.vector.tensor_copy(y3[:], y[:].indirect(n3_t[:]))
+            if t + 2 < PACK:
+                w_packed.append(quantise_w(t + 2))
             nc.vector.tensor_tensor(left[:, t, :], y_scaled[:].indirect(n2_t[:]), y1[:], ALU.mult)
             nc.vector.tensor_tensor(right[:, t, :], y_scaled[:].indirect(n4_t[:]), y3[:], ALU.mult)
 
-        empty_y(0, project(0))
+        project(0)
         for t in range(PACK):
             if t + 1 < PACK:
-                empty_y(t + 1, project(t + 1))
+                project(t + 1)
             look_up_y(t)
 
         s_banks = [psum.tile([P, S], F32, name=f"s_bank{u}") for u in range(PACK)]
@@ -159,38 +163,43 @@ def tile_picked_canddetminmx_none_p_kernel(
             )
             return z_bf
 
-        def score(lo, hi, z_bf):
+        def score(u, lo, hi):
+            words, scale_bytes = dealt[u]
+            nc.tensor.matmul_mx(
+                out=s_banks[u][:, lo:hi],
+                lhsT=words.bitcast(FP8X4),
+                lhsT_scale=scale_bytes,
+                rhs=z_words[:, lo:hi].bitcast(FP8X4),
+                rhs_scale=z_bytes[:, lo:hi],
+                start=True,
+                stop=True,
+            )
+            nc.scalar.activation(windows[u][:, lo:hi], s_banks[u][:, lo:hi], COPY, scale=0.0625)
+
+        def quantise_z(lo, hi, z_bf):
             nc.vector.quantize_mx(
                 out=z_words[:, lo:hi].bitcast(FP8X4), scales=z_bytes[:, lo:hi], in_=z_bf[:]
             )
-            for u in range(PACK):
-                nc.tensor.matmul_mx(
-                    out=s_banks[u][:, lo:hi],
-                    lhsT=dealt_words[:, P * u : P * (u + 1)].bitcast(FP8X4),
-                    lhsT_scale=dealt_bytes[:, P * u : P * (u + 1)],
-                    rhs=z_words[:, lo:hi].bitcast(FP8X4),
-                    rhs_scale=z_bytes[:, lo:hi],
-                    start=True,
-                    stop=True,
-                )
-            nc.scalar.activation(windows[0][:, lo:hi], s_banks[0][:, lo:hi], COPY, scale=0.0625)
+            score(0, lo, hi)
 
+        dealt = deal("first", 0, 1)
         pending = None
         for lo, hi in Z_PIECES:
             z_bf = subtract(lo, hi)
             if pending is not None:
-                score(*pending)
+                quantise_z(*pending)
             pending = (lo, hi, z_bf)
-        score(*pending)
+        quantise_z(*pending)
+        dealt.extend(deal("rest", 1, PACK - 1))
         for u in range(1, PACK):
-            nc.scalar.activation(windows[u][:, :S], s_banks[u][:], COPY, scale=0.0625)
+            score(u, 0, S)
 
         out_rows = out.rearrange("(p u) j -> p u j", u=PACK)
 
-        def finish(u, larger, s6):
-            result = keep.tile([P, S], F32, name=f"result{u}")
-            nc.vector.tensor_tensor(result[:], larger[:], s6[:], ALU.min)
-            nc.sync.dma_start(out_rows[:, u, :], result[:])
+        def finish(u, larger, s6, lo, hi):
+            result = keep.tile([P, hi - lo], F32, name=f"result{u}_{lo}")
+            nc.vector.tensor_tensor(result[:], larger[:, lo:hi], s6[:, lo:hi], ALU.min)
+            nc.sync.dma_start(out_rows[:, u, lo:hi], result[:])
 
         pending = None
         for u in range(PACK):
@@ -200,8 +209,15 @@ def tile_picked_canddetminmx_none_p_kernel(
             larger = ring.tile([P, S], F32, name="larger")
             nc.vector.tensor_copy(s5[:], s[:].indirect(n5_t[:]))
             if pending is not None:
-                finish(*pending)
-            nc.vector.tensor_copy(s6[:], s[:].indirect(n6_t[:]))
-            nc.vector.tensor_tensor(larger[:], s5[:], s[:, :S], ALU.max)
+                finish(*pending, 0, S)
+            if u + 1 < PACK:
+                nc.vector.tensor_copy(s6[:], s[:].indirect(n6_t[:]))
+                nc.vector.tensor_tensor(larger[:], s5[:], s[:, :S], ALU.max)
+            else:
+                nc.vector.tensor_tensor(larger[:], s5[:], s[:, :S], ALU.max)
+                for lo in (0, S // 2):
+                    hi = lo + S // 2
+                    nc.vector.tensor_copy(s6[:, lo:hi], s[:].indirect(n6_t[:, lo // 16 : hi // 16]))
             pending = (u, larger, s6)
-        finish(*pending)
+        for lo in (0, S // 2):
+            finish(*pending, lo, lo + S // 2)

@@ -54,8 +54,8 @@ def tile_picked_canddetminmx_none_p_kernel(
         n1_t = load_list("n1_t", n1)
         gs_raw = keep.tile([P, PACK], F32, name="gs_raw")
         nc.sync.dma_start(gs_raw[:], gs.rearrange("(p t) o -> p (t o)", t=PACK))
-        n3_t = load_list("n3_t", n3)
         n2_t = load_list("n2_t", n2)
+        n3_t = load_list("n3_t", n3)
         n4_t = load_list("n4_t", n4)
         n5_t = load_list("n5_t", n5)
         n6_t = load_list("n6_t", n6)
@@ -92,9 +92,9 @@ def tile_picked_canddetminmx_none_p_kernel(
             )
             return w_words, w_bytes
 
-        def deal(name, first, count):
-            words = keep.tile([P, count, P], U32, name=name + "_words", align_bytes=64)
-            scale_bytes = keep.tile([P, count, P], U8, name=name + "_bytes", align_bytes=64)
+        def deal(words_tag, bytes_tag, first, count):
+            words = keep.tile([P, count, P], U32, name=words_tag, align_bytes=64)
+            scale_bytes = keep.tile([P, count, P], U8, name=bytes_tag, align_bytes=64)
             nc.vector.tensor_copy(
                 scale_bytes[:], xc_bytes[:].rearrange("p (m u) -> p u m", u=PACK)[:, first : first + count, :]
             )
@@ -111,8 +111,8 @@ def tile_picked_canddetminmx_none_p_kernel(
         xc_words = gather_words("xc_words", cand_t)
 
         gs_scaled = keep.tile([P, PACK], F32, name="gs_scaled")
-        left = keep.tile([P, PACK, S], F32, name="left")
-        right = keep.tile([P, PACK, S], F32, name="right")
+        left = keep.tile([P, PACK, S], F32, name="left", align_bytes=64)
+        right = keep.tile([P, PACK, S], F32, name="right", align_bytes=64)
 
         def project(t):
             w_words, w_bytes = w_packed[t]
@@ -136,12 +136,19 @@ def tile_picked_canddetminmx_none_p_kernel(
             y, y_scaled = windows[2 * (t % 2)], windows[2 * (t % 2) + 1]
             y1 = ring.tile([P, S], F32, name="y1")
             y3 = ring.tile([P, S], F32, name="y3")
-            nc.vector.tensor_copy(y1[:], y[:].indirect(n1_t[:]))
-            nc.vector.tensor_copy(y3[:], y[:].indirect(n3_t[:]))
+            y2 = ring.tile([P, S], F32, name="y2")
             if t + 2 < PACK:
                 w_packed.append(quantise_w(t + 2))
-            nc.vector.tensor_tensor(left[:, t, :], y_scaled[:].indirect(n2_t[:]), y1[:], ALU.mult)
-            nc.vector.tensor_tensor(right[:, t, :], y_scaled[:].indirect(n4_t[:]), y3[:], ALU.mult)
+            nc.vector.tensor_copy(y1[:], y[:].indirect(n1_t[:]))
+            nc.vector.tensor_copy(y2[:], y_scaled[:].indirect(n2_t[:]))
+            nc.gpsimd.tensor_tensor(left[:, t, :], y2[:], y1[:], ALU.mult)
+            nc.vector.tensor_copy(y3[:], y[:].indirect(n3_t[:]))
+            if t + 1 < PACK:
+                y4 = ring.tile([P, S], F32, name="y4")
+                nc.vector.tensor_copy(y4[:], y_scaled[:].indirect(n4_t[:]))
+                nc.gpsimd.tensor_tensor(right[:, t, :], y4[:], y3[:], ALU.mult)
+            else:
+                nc.vector.tensor_tensor(right[:, t, :], y_scaled[:].indirect(n4_t[:]), y3[:], ALU.mult)
 
         project(0)
         for t in range(PACK):
@@ -182,7 +189,7 @@ def tile_picked_canddetminmx_none_p_kernel(
             )
             score(0, lo, hi)
 
-        dealt = deal("first", 0, 1)
+        dealt = deal("first_words", "first_bytes", 0, 1)
         pending = None
         for lo, hi in Z_PIECES:
             z_bf = subtract(lo, hi)
@@ -190,7 +197,7 @@ def tile_picked_canddetminmx_none_p_kernel(
                 quantise_z(*pending)
             pending = (lo, hi, z_bf)
         quantise_z(*pending)
-        dealt.extend(deal("rest", 1, PACK - 1))
+        dealt.extend(deal("left", "right", 1, PACK - 1))
         for u in range(1, PACK):
             score(u, 0, S)
 

@@ -18,7 +18,6 @@ COPY = mybir.ActivationFunctionType.Copy
 P = 128
 PACK = 4
 WINDOW = 2 * S
-Z_PIECES = ((0, 256), (256, 384), (384, 512))
 
 
 def tile_picked_canddetminmx_none_p_kernel(
@@ -54,8 +53,8 @@ def tile_picked_canddetminmx_none_p_kernel(
         n1_t = load_list("n1_t", n1)
         gs_raw = keep.tile([P, PACK], F32, name="gs_raw")
         nc.sync.dma_start(gs_raw[:], gs.rearrange("(p t) o -> p (t o)", t=PACK))
-        n2_t = load_list("n2_t", n2)
         n3_t = load_list("n3_t", n3)
+        n2_t = load_list("n2_t", n2)
         n4_t = load_list("n4_t", n4)
         n5_t = load_list("n5_t", n5)
         n6_t = load_list("n6_t", n6)
@@ -92,27 +91,24 @@ def tile_picked_canddetminmx_none_p_kernel(
             )
             return w_words, w_bytes
 
-        def deal(words_tag, bytes_tag, first, count):
-            words = keep.tile([P, count, P], U32, name=words_tag, align_bytes=64)
-            scale_bytes = keep.tile([P, count, P], U8, name=bytes_tag, align_bytes=64)
-            nc.vector.tensor_copy(
-                scale_bytes[:], xc_bytes[:].rearrange("p (m u) -> p u m", u=PACK)[:, first : first + count, :]
-            )
+        def deal_words(tag, first, count):
+            words = keep.tile([P, count, P], U32, name=tag, align_bytes=64)
             nc.vector.tensor_copy(
                 words[:].rearrange("p u (c i) -> p c u i", i=4),
                 xc_words[:].rearrange("p (c i u) -> p c u i", u=PACK, i=4)[:, :, first : first + count, :],
             )
-            return [(words[:, u, :], scale_bytes[:, u, :]) for u in range(count)]
+            return [words[:, u, :] for u in range(count)]
 
         xq_bytes = gather_bytes("xq_bytes", offs_t)
         xc_bytes = gather_bytes("xc_bytes", cand_t)
         w_packed = [quantise_w(0), quantise_w(1)]
+        dealt_bytes = keep.tile([P, PACK, P], U8, name="dealt_bytes", align_bytes=64)
+        nc.vector.tensor_copy(dealt_bytes[:], xc_bytes[:].rearrange("p (m u) -> p u m", u=PACK))
         xq_words = gather_words("xq_words", offs_t)
         xc_words = gather_words("xc_words", cand_t)
 
         gs_scaled = keep.tile([P, PACK], F32, name="gs_scaled")
-        left = keep.tile([P, PACK, S], F32, name="left", align_bytes=64)
-        right = keep.tile([P, PACK, S], F32, name="right", align_bytes=64)
+        z = keep.tile([P, PACK, S], F32, name="z")
 
         def project(t):
             w_words, w_bytes = w_packed[t]
@@ -134,21 +130,21 @@ def tile_picked_canddetminmx_none_p_kernel(
 
         def look_up_y(t):
             y, y_scaled = windows[2 * (t % 2)], windows[2 * (t % 2) + 1]
-            y1 = ring.tile([P, S], F32, name="y1")
-            y3 = ring.tile([P, S], F32, name="y3")
-            y2 = ring.tile([P, S], F32, name="y2")
+            y1 = keep.tile([P, S], F32, name="y1")
+            y3 = keep.tile([P, S], F32, name="y3")
+            left = ring.tile([P, S], F32, name="left")
+            right = ring.tile([P, S], F32, name="right")
             if t + 2 < PACK:
                 w_packed.append(quantise_w(t + 2))
             nc.vector.tensor_copy(y1[:], y[:].indirect(n1_t[:]))
-            nc.vector.tensor_copy(y2[:], y_scaled[:].indirect(n2_t[:]))
-            nc.gpsimd.tensor_tensor(left[:, t, :], y2[:], y1[:], ALU.mult)
             nc.vector.tensor_copy(y3[:], y[:].indirect(n3_t[:]))
+            nc.vector.tensor_tensor(left[:], y_scaled[:].indirect(n2_t[:]), y1[:], ALU.mult)
+            nc.vector.tensor_tensor(right[:], y_scaled[:].indirect(n4_t[:]), y3[:], ALU.mult)
             if t + 1 < PACK:
-                y4 = ring.tile([P, S], F32, name="y4")
-                nc.vector.tensor_copy(y4[:], y_scaled[:].indirect(n4_t[:]))
-                nc.gpsimd.tensor_tensor(right[:, t, :], y4[:], y3[:], ALU.mult)
+                nc.gpsimd.tensor_tensor(z[:, t, :], left[:], right[:], ALU.subtract)
             else:
-                nc.vector.tensor_tensor(right[:, t, :], y_scaled[:].indirect(n4_t[:]), y3[:], ALU.mult)
+                for half in (slice(0, S // 2), slice(S // 2, S)):
+                    nc.vector.tensor_tensor(z[:, t, half], left[:, half], right[:, half], ALU.subtract)
 
         project(0)
         for t in range(PACK):
@@ -160,22 +156,16 @@ def tile_picked_canddetminmx_none_p_kernel(
         z_words = keep.tile([P, S], U32, name="z_words", align_bytes=64)
         z_bytes = keep.tile([P, S], U8, name="z_bytes", align_bytes=64)
 
-        def subtract(lo, hi):
-            z_bf = keep.tile([P, (hi - lo) * PACK], BF16, name=f"z_bf{lo}", align_bytes=64)
-            nc.vector.tensor_tensor(
-                z_bf[:].rearrange("p (c i t) -> p c t i", i=2, t=PACK),
-                left[:, :, lo:hi].rearrange("p t (c i) -> p c t i", i=2),
-                right[:, :, lo:hi].rearrange("p t (c i) -> p c t i", i=2),
-                ALU.subtract,
-            )
+        def round_z(copy, lo, hi):
+            z_bf = keep.tile([P, hi - lo, PACK], BF16, name=f"z_bf{lo}", align_bytes=64)
+            copy(z_bf[:], z[:, :, lo:hi].rearrange("p t c -> p c t"))
             return z_bf
 
         def score(u, lo, hi):
-            words, scale_bytes = dealt[u]
             nc.tensor.matmul_mx(
                 out=s_banks[u][:, lo:hi],
-                lhsT=words.bitcast(FP8X4),
-                lhsT_scale=scale_bytes,
+                lhsT=dealt_words[u].bitcast(FP8X4),
+                lhsT_scale=dealt_bytes[:, u, :],
                 rhs=z_words[:, lo:hi].bitcast(FP8X4),
                 rhs_scale=z_bytes[:, lo:hi],
                 start=True,
@@ -185,19 +175,20 @@ def tile_picked_canddetminmx_none_p_kernel(
 
         def quantise_z(lo, hi, z_bf):
             nc.vector.quantize_mx(
-                out=z_words[:, lo:hi].bitcast(FP8X4), scales=z_bytes[:, lo:hi], in_=z_bf[:]
+                out=z_words[:, lo:hi].bitcast(FP8X4), scales=z_bytes[:, lo:hi], in_=z_bf[:].rearrange("p c t -> p (c t)")
             )
             score(0, lo, hi)
 
-        dealt = deal("first_words", "first_bytes", 0, 1)
-        pending = None
-        for lo, hi in Z_PIECES:
-            z_bf = subtract(lo, hi)
-            if pending is not None:
-                quantise_z(*pending)
-            pending = (lo, hi, z_bf)
-        quantise_z(*pending)
-        dealt.extend(deal("left", "right", 1, PACK - 1))
+        dealt_words = deal_words("first_words", 0, 1)
+        pieces = (
+            (nc.scalar.copy, 0, 128),
+            (nc.vector.tensor_copy, 256, 512),
+            (nc.scalar.copy, 128, 256),
+        )
+        rounded = [round_z(*piece) for piece in pieces]
+        for (copy, lo, hi), z_bf in zip(pieces, rounded):
+            quantise_z(lo, hi, z_bf)
+        dealt_words.extend(deal_words("z_bf128", 1, PACK - 1))
         for u in range(1, PACK):
             score(u, 0, S)
 

@@ -18,6 +18,7 @@ COPY = mybir.ActivationFunctionType.Copy
 P = 128
 PACK = 4
 WINDOW = 2 * S
+HALVES = (slice(0, S // 2), slice(S // 2, S))
 
 
 def tile_picked_canddetminmx_none_p_kernel(
@@ -35,8 +36,7 @@ def tile_picked_canddetminmx_none_p_kernel(
             return tile
 
         table_bytes = keep.tile([P, T], U8, name="table_bytes", align_bytes=64)
-        nc.vector.memset(table_bytes[:, : T // 2].bitcast(I32), 0)
-        nc.gpsimd.memset(table_bytes[:, T // 2 :].bitcast(I32), 0)
+        nc.vector.memset(table_bytes[:].bitcast(I32), 0)
         offs_t = load_list("offs_t", offs)
         w_rows = w1.rearrange("(p j) c -> p j c", j=PACK)
         w_raw = [keep.tile([P, PACK, H // 2], F32, name=f"w_raw{h}") for h in range(2)]
@@ -70,72 +70,69 @@ def tile_picked_canddetminmx_none_p_kernel(
             nc.vector.tensor_copy(scale_bytes[:], table_bytes[:].indirect(offsets[:]))
             return scale_bytes
 
-        def gather_words(name, offsets):
-            words = keep.tile([P, S], U32, name=name, align_bytes=64)
-            nc.vector.tensor_copy(words[:], table_words[:].bitcast(U32).indirect(offsets[:]))
+        def gather_words(tag, offsets):
+            words = keep.tile([P, 16 * offsets.shape[1]], U32, name=tag, align_bytes=64)
+            nc.vector.tensor_copy(words[:], table_words[:].bitcast(U32).indirect(offsets))
             return words
 
-        def quantise_w(t):
-            w_bf = ring.tile([P, P, PACK], BF16, name="w_bf", align_bytes=64)
-            for h in range(2):
-                nc.scalar.copy(
-                    w_bf[:, 64 * h : 64 * (h + 1), :],
-                    w_raw[h][:].rearrange("p j (m t) -> p t m j", t=PACK)[:, t],
-                )
-            w_words = ring.tile([P, P], U32, name="w_words", align_bytes=64)
-            w_bytes = ring.tile([P, P], U8, name="w_bytes", align_bytes=64)
-            nc.vector.quantize_mx(
-                out=w_words[:].bitcast(FP8X4),
-                scales=w_bytes[:],
-                in_=w_bf[:].rearrange("p m j -> p (m j)"),
-            )
-            return w_words, w_bytes
-
-        def deal_words(tag, first, count):
-            words = keep.tile([P, count, P], U32, name=tag, align_bytes=64)
+        def deal(words_tag, bytes_tag, first, count):
+            words = keep.tile([P, count, P], U32, name=words_tag, align_bytes=64)
+            scale_bytes = keep.tile([P, count, P], U8, name=bytes_tag, align_bytes=64)
             nc.vector.tensor_copy(
                 words[:].rearrange("p u (c i) -> p c u i", i=4),
                 xc_words[:].rearrange("p (c i u) -> p c u i", u=PACK, i=4)[:, :, first : first + count, :],
             )
-            return [words[:, u, :] for u in range(count)]
+            nc.vector.tensor_copy(
+                scale_bytes[:], xc_bytes[:].rearrange("p (m u) -> p u m", u=PACK)[:, first : first + count, :]
+            )
+            return [(words[:, u, :], scale_bytes[:, u, :]) for u in range(count)]
 
         xq_bytes = gather_bytes("xq_bytes", offs_t)
         xc_bytes = gather_bytes("xc_bytes", cand_t)
-        w_packed = [quantise_w(0), quantise_w(1)]
-        dealt_bytes = keep.tile([P, PACK, P], U8, name="dealt_bytes", align_bytes=64)
-        nc.vector.tensor_copy(dealt_bytes[:], xc_bytes[:].rearrange("p (m u) -> p u m", u=PACK))
-        xq_words = gather_words("xq_words", offs_t)
-        xc_words = gather_words("xc_words", cand_t)
+        w_bf = keep.tile([P, PACK, P, PACK], BF16, name="w_bf", align_bytes=64)
+        for h in range(2):
+            nc.scalar.copy(
+                w_bf[:, :, h * (P // 2) : (h + 1) * (P // 2), :].rearrange("p t m j -> p m t j"),
+                w_raw[h][:].rearrange("p j (m t) -> p m t j", t=PACK),
+            )
+        w_words = keep.tile([P, PACK, P], U32, name="w_words", align_bytes=64)
+        w_bytes = keep.tile([P, PACK, P], U8, name="w_bytes", align_bytes=64)
+        nc.vector.quantize_mx(
+            out=w_words[:].rearrange("p t m -> p (t m)").bitcast(FP8X4),
+            scales=w_bytes[:].rearrange("p t m -> p (t m)"),
+            in_=w_bf[:].rearrange("p t m j -> p (t m j)"),
+        )
+        xq_words = [gather_words("w_bf", offs_t[:, :16]), gather_words("xq_words", offs_t[:, 16:])]
+        xc_words = gather_words("xc_words", cand_t[:])
 
         gs_scaled = keep.tile([P, PACK], F32, name="gs_scaled")
         z = keep.tile([P, PACK, S], F32, name="z")
 
         def project(t):
-            w_words, w_bytes = w_packed[t]
-            y_bank = psum.tile([P, S], F32, name=f"y_bank{t}")
-            nc.tensor.matmul_mx(
-                out=y_bank[:],
-                lhsT=w_words[:].bitcast(FP8X4),
-                lhsT_scale=w_bytes[:],
-                rhs=xq_words[:].bitcast(FP8X4),
-                rhs_scale=xq_bytes[:],
-                start=True,
-                stop=True,
-            )
             y, y_scaled = windows[2 * (t % 2)], windows[2 * (t % 2) + 1]
-            nc.scalar.copy(y[:, :S], y_bank[:])
+            banks = [psum.tile([P, S // 2], F32, name=f"bank{2 * (t % 2) + h}") for h in range(2)]
+            for h, half in enumerate(HALVES):
+                nc.tensor.matmul_mx(
+                    out=banks[h][:],
+                    lhsT=w_words[:, t, :].bitcast(FP8X4),
+                    lhsT_scale=w_bytes[:, t, :],
+                    rhs=xq_words[h][:].bitcast(FP8X4),
+                    rhs_scale=xq_bytes[:, half],
+                    start=True,
+                    stop=True,
+                )
+                nc.scalar.copy(y[:, half], banks[h][:])
             if t == 0:
                 nc.scalar.activation(gs_scaled[:], gs_raw[:], COPY, scale=0.75)
-            nc.scalar.activation(y_scaled[:, :S], y_bank[:], COPY, scale=gs_scaled[:, t : t + 1])
+            for h, half in enumerate(HALVES):
+                nc.scalar.activation(y_scaled[:, half], banks[h][:], COPY, scale=gs_scaled[:, t : t + 1])
 
         def look_up_y(t):
             y, y_scaled = windows[2 * (t % 2)], windows[2 * (t % 2) + 1]
-            y1 = keep.tile([P, S], F32, name="y1")
-            y3 = keep.tile([P, S], F32, name="y3")
+            y1 = keep.tile([P, S], F32, name="y1", align_bytes=64)
+            y3 = keep.tile([P, S], F32, name="y3", align_bytes=64)
             left = ring.tile([P, S], F32, name="left")
             right = ring.tile([P, S], F32, name="right")
-            if t + 2 < PACK:
-                w_packed.append(quantise_w(t + 2))
             nc.vector.tensor_copy(y1[:], y[:].indirect(n1_t[:]))
             nc.vector.tensor_copy(y3[:], y[:].indirect(n3_t[:]))
             nc.vector.tensor_tensor(left[:], y_scaled[:].indirect(n2_t[:]), y1[:], ALU.mult)
@@ -143,9 +140,11 @@ def tile_picked_canddetminmx_none_p_kernel(
             if t + 1 < PACK:
                 nc.gpsimd.tensor_tensor(z[:, t, :], left[:], right[:], ALU.subtract)
             else:
-                for half in (slice(0, S // 2), slice(S // 2, S)):
-                    nc.vector.tensor_tensor(z[:, t, half], left[:, half], right[:, half], ALU.subtract)
+                dealt.extend(deal("y1", "y3", 0, 1))
+                for cols in (slice(0, 128), slice(128, S)):
+                    nc.vector.tensor_tensor(z[:, t, cols], left[:, cols], right[:, cols], ALU.subtract)
 
+        dealt = []
         project(0)
         for t in range(PACK):
             if t + 1 < PACK:
@@ -164,8 +163,8 @@ def tile_picked_canddetminmx_none_p_kernel(
         def score(u, lo, hi):
             nc.tensor.matmul_mx(
                 out=s_banks[u][:, lo:hi],
-                lhsT=dealt_words[u].bitcast(FP8X4),
-                lhsT_scale=dealt_bytes[:, u, :],
+                lhsT=dealt[u][0].bitcast(FP8X4),
+                lhsT_scale=dealt[u][1],
                 rhs=z_words[:, lo:hi].bitcast(FP8X4),
                 rhs_scale=z_bytes[:, lo:hi],
                 start=True,
@@ -179,7 +178,6 @@ def tile_picked_canddetminmx_none_p_kernel(
             )
             score(0, lo, hi)
 
-        dealt_words = deal_words("first_words", 0, 1)
         pieces = (
             (nc.scalar.copy, 0, 128),
             (nc.vector.tensor_copy, 256, 512),
@@ -188,34 +186,22 @@ def tile_picked_canddetminmx_none_p_kernel(
         rounded = [round_z(*piece) for piece in pieces]
         for (copy, lo, hi), z_bf in zip(pieces, rounded):
             quantise_z(lo, hi, z_bf)
-        dealt_words.extend(deal_words("z_bf128", 1, PACK - 1))
+        dealt.extend(deal("z_bf128", "z_bf256", 1, PACK - 1))
         for u in range(1, PACK):
             score(u, 0, S)
 
         out_rows = out.rearrange("(p u) j -> p u j", u=PACK)
 
-        def finish(u, larger, s6, lo, hi):
-            result = keep.tile([P, hi - lo], F32, name=f"result{u}_{lo}")
-            nc.vector.tensor_tensor(result[:], larger[:, lo:hi], s6[:, lo:hi], ALU.min)
-            nc.sync.dma_start(out_rows[:, u, lo:hi], result[:])
-
-        pending = None
         for u in range(PACK):
             s = windows[u]
             s5 = ring.tile([P, S], F32, name="s5")
             s6 = ring.tile([P, S], F32, name="s6")
             larger = ring.tile([P, S], F32, name="larger")
+            result = keep.tile([P, S], F32, name=f"result{u}")
             nc.vector.tensor_copy(s5[:], s[:].indirect(n5_t[:]))
-            if pending is not None:
-                finish(*pending, 0, S)
-            if u + 1 < PACK:
-                nc.vector.tensor_copy(s6[:], s[:].indirect(n6_t[:]))
-                nc.vector.tensor_tensor(larger[:], s5[:], s[:, :S], ALU.max)
-            else:
-                nc.vector.tensor_tensor(larger[:], s5[:], s[:, :S], ALU.max)
-                for lo in (0, S // 2):
-                    hi = lo + S // 2
-                    nc.vector.tensor_copy(s6[:, lo:hi], s[:].indirect(n6_t[:, lo // 16 : hi // 16]))
-            pending = (u, larger, s6)
-        for lo in (0, S // 2):
-            finish(*pending, lo, lo + S // 2)
+            nc.vector.tensor_copy(s6[:], s[:].indirect(n6_t[:]))
+            for half in HALVES:
+                nc.vector.tensor_tensor(larger[:, half], s5[:, half], s[:, half], ALU.max)
+            for half in HALVES:
+                nc.vector.tensor_tensor(result[:, half], larger[:, half], s6[:, half], ALU.min)
+                nc.sync.dma_start(out_rows[:, u, half], result[:, half])

from contextlib import ExitStack

import concourse.mybir as mybir

K, T, S, H, C = 512, 2048, 512, 512, 512
FLOPS = 2 * K * H * S + 2 * K * C * S

F32 = mybir.dt.float32
BF16 = mybir.dt.bfloat16
I32 = mybir.dt.int32
U32 = mybir.dt.uint32
U16 = mybir.dt.uint16
U8 = mybir.dt.uint8
FP8X4 = mybir.dt.float8_e4m3fn_x4
ALU = mybir.AluOpType
COPY = mybir.ActivationFunctionType.Copy

P = 128
PACK = 4
WINDOW = 2 * S
HALVES = (slice(0, S // 2), slice(S // 2, S))


def tile_picked_canddetminmx_none_p_kernel(
    tc, x_words, x_scales, w1, gs, offs, n1, n2, n3, n4, cand, n5, n6, out
):
    nc = tc.nc
    with ExitStack() as ctx:
        keep = ctx.enter_context(tc.tile_pool(name="keep", bufs=1))
        ring = ctx.enter_context(tc.tile_pool(name="ring", bufs=2))
        psum = ctx.enter_context(tc.psum_pool(name="psum", bufs=1))

        def load_list(name, source):
            tile = keep.tile([P, S // 16], U16, name=name)
            nc.sync.dma_start(tile[:], source)
            return tile

        table_bytes = keep.tile([P, T], U8, name="table_bytes", align_bytes=64)
        nc.vector.memset(table_bytes[:].bitcast(I32), 0)
        offs_t = load_list("offs_t", offs)
        w_rows = w1.rearrange("(p j) c -> p j c", j=PACK)
        w_raw = [keep.tile([P, PACK, H // 2], F32, name=f"w_raw{h}") for h in range(2)]
        nc.sync.dma_start(w_raw[0][:], w_rows[:, :, : H // 2])
        cand_t = load_list("cand_t", cand)
        for q in range(4):
            nc.sync.dma_start(
                table_bytes[32 * q : 32 * q + 4, :].bitcast(I32),
                x_scales[0, 4 * q : 4 * q + 4, :].bitcast(I32),
            )
        nc.sync.dma_start(w_raw[1][:], w_rows[:, :, H // 2 :])
        table_words = keep.tile([P, T], I32, name="table_words", align_bytes=64)
        nc.sync.dma_start(table_words[:], x_words[0].rearrange("p n r -> p (n r)").bitcast(I32))
        n1_t = load_list("n1_t", n1)
        gs_raw = keep.tile([P, PACK], F32, name="gs_raw")
        nc.sync.dma_start(gs_raw[:], gs.rearrange("(p t) o -> p (t o)", t=PACK))
        n3_t = load_list("n3_t", n3)
        n2_t = load_list("n2_t", n2)
        n4_t = load_list("n4_t", n4)
        n5_t = load_list("n5_t", n5)
        n6_t = load_list("n6_t", n6)

        windows = []
        for w in range(4):
            window = keep.tile([P, WINDOW], F32, name=f"window{w}")
            nc.gpsimd.memset(window[:, S:], 0.0)
            windows.append(window)

        def gather_bytes(name, offsets):
            scale_bytes = keep.tile([P, S], U8, name=name, align_bytes=64)
            nc.vector.tensor_copy(scale_bytes[:], table_bytes[:].indirect(offsets[:]))
            return scale_bytes

        def gather_words(tag, offsets):
            words = keep.tile([P, 16 * offsets.shape[1]], U32, name=tag, align_bytes=64)
            nc.vector.tensor_copy(words[:], table_words[:].bitcast(U32).indirect(offsets))
            return words

        def deal(words_tag, bytes_tag, first, count):
            words = keep.tile([P, count, P], U32, name=words_tag, align_bytes=64)
            scale_bytes = keep.tile([P, count, P], U8, name=bytes_tag, align_bytes=64)
            nc.vector.tensor_copy(
                words[:].rearrange("p u (c i) -> p c u i", i=4),
                xc_words[:].rearrange("p (c i u) -> p c u i", u=PACK, i=4)[:, :, first : first + count, :],
            )
            nc.vector.tensor_copy(
                scale_bytes[:], xc_bytes[:].rearrange("p (m u) -> p u m", u=PACK)[:, first : first + count, :]
            )
            return [(words[:, u, :], scale_bytes[:, u, :]) for u in range(count)]

        xq_bytes = gather_bytes("xq_bytes", offs_t)
        xc_bytes = gather_bytes("xc_bytes", cand_t)
        w_bf = keep.tile([P, PACK, P, PACK], BF16, name="w_bf", align_bytes=64)
        for h in range(2):
            nc.scalar.copy(
                w_bf[:, :, h * (P // 2) : (h + 1) * (P // 2), :].rearrange("p t m j -> p m t j"),
                w_raw[h][:].rearrange("p j (m t) -> p m t j", t=PACK),
            )
        w_words = keep.tile([P, PACK, P], U32, name="w_words", align_bytes=64)
        w_bytes = keep.tile([P, PACK, P], U8, name="w_bytes", align_bytes=64)
        nc.vector.quantize_mx(
            out=w_words[:].rearrange("p t m -> p (t m)").bitcast(FP8X4),
            scales=w_bytes[:].rearrange("p t m -> p (t m)"),
            in_=w_bf[:].rearrange("p t m j -> p (t m j)"),
        )
        xq_words = [gather_words("w_bf", offs_t[:, :16]), gather_words("xq_words", offs_t[:, 16:])]
        xc_words = gather_words("xc_words", cand_t[:])

        gs_scaled = keep.tile([P, PACK], F32, name="gs_scaled")
        z = keep.tile([P, PACK, S], F32, name="z")

        def project(t):
            y, y_scaled = windows[2 * (t % 2)], windows[2 * (t % 2) + 1]
            banks = [psum.tile([P, S // 2], F32, name=f"bank{2 * (t % 2) + h}") for h in range(2)]
            for h, half in enumerate(HALVES):
                nc.tensor.matmul_mx(
                    out=banks[h][:],
                    lhsT=w_words[:, t, :].bitcast(FP8X4),
                    lhsT_scale=w_bytes[:, t, :],
                    rhs=xq_words[h][:].bitcast(FP8X4),
                    rhs_scale=xq_bytes[:, half],
                    start=True,
                    stop=True,
                )
                nc.scalar.copy(y[:, half], banks[h][:])
            if t == 0:
                nc.scalar.activation(gs_scaled[:], gs_raw[:], COPY, scale=0.75)
            for h, half in enumerate(HALVES):
                nc.scalar.activation(y_scaled[:, half], banks[h][:], COPY, scale=gs_scaled[:, t : t + 1])

        def look_up_y(t):
            y, y_scaled = windows[2 * (t % 2)], windows[2 * (t % 2) + 1]
            y1 = keep.tile([P, S], F32, name="y1", align_bytes=64)
            y3 = keep.tile([P, S], F32, name="y3", align_bytes=64)
            left = ring.tile([P, S], F32, name="left")
            right = ring.tile([P, S], F32, name="right")
            nc.vector.tensor_copy(y1[:], y[:].indirect(n1_t[:]))
            nc.vector.tensor_copy(y3[:], y[:].indirect(n3_t[:]))
            nc.vector.tensor_tensor(left[:], y_scaled[:].indirect(n2_t[:]), y1[:], ALU.mult)
            nc.vector.tensor_tensor(right[:], y_scaled[:].indirect(n4_t[:]), y3[:], ALU.mult)
            if t + 1 < PACK:
                nc.gpsimd.tensor_tensor(z[:, t, :], left[:], right[:], ALU.subtract)
            else:
                dealt.extend(deal("y1", "y3", 0, 1))
                for cols in (slice(0, 128), slice(128, S)):
                    nc.vector.tensor_tensor(z[:, t, cols], left[:, cols], right[:, cols], ALU.subtract)

        dealt = []
        project(0)
        for t in range(PACK):
            if t + 1 < PACK:
                project(t + 1)
            look_up_y(t)

        s_banks = [psum.tile([P, S], F32, name=f"s_bank{u}") for u in range(PACK)]
        z_words = keep.tile([P, S], U32, name="z_words", align_bytes=64)
        z_bytes = keep.tile([P, S], U8, name="z_bytes", align_bytes=64)

        def round_z(copy, lo, hi):
            z_bf = keep.tile([P, hi - lo, PACK], BF16, name=f"z_bf{lo}", align_bytes=64)
            copy(z_bf[:], z[:, :, lo:hi].rearrange("p t c -> p c t"))
            return z_bf

        def score(u, lo, hi):
            nc.tensor.matmul_mx(
                out=s_banks[u][:, lo:hi],
                lhsT=dealt[u][0].bitcast(FP8X4),
                lhsT_scale=dealt[u][1],
                rhs=z_words[:, lo:hi].bitcast(FP8X4),
                rhs_scale=z_bytes[:, lo:hi],
                start=True,
                stop=True,
            )
            nc.scalar.activation(windows[u][:, lo:hi], s_banks[u][:, lo:hi], COPY, scale=0.0625)

        def quantise_z(lo, hi, z_bf):
            nc.vector.quantize_mx(
                out=z_words[:, lo:hi].bitcast(FP8X4), scales=z_bytes[:, lo:hi], in_=z_bf[:].rearrange("p c t -> p (c t)")
            )
            score(0, lo, hi)

        pieces = (
            (nc.scalar.copy, 0, 128),
            (nc.vector.tensor_copy, 256, 512),
            (nc.scalar.copy, 128, 256),
        )
        rounded = [round_z(*piece) for piece in pieces]
        for (copy, lo, hi), z_bf in zip(pieces, rounded):
            quantise_z(lo, hi, z_bf)
        dealt.extend(deal("z_bf128", "z_bf256", 1, PACK - 1))
        for u in range(1, PACK):
            score(u, 0, S)

        out_rows = out.rearrange("(p u) j -> p u j", u=PACK)

        for u in range(PACK):
            s = windows[u]
            s5 = ring.tile([P, S], F32, name="s5")
            s6 = ring.tile([P, S], F32, name="s6")
            larger = ring.tile([P, S], F32, name="larger")
            result = keep.tile([P, S], F32, name=f"result{u}")
            nc.vector.tensor_copy(s5[:], s[:].indirect(n5_t[:]))
            nc.vector.tensor_copy(s6[:], s[:].indirect(n6_t[:]))
            for half in HALVES:
                nc.vector.tensor_tensor(larger[:, half], s5[:, half], s[:, half], ALU.max)
            for half in HALVES:
                nc.vector.tensor_tensor(result[:, half], larger[:, half], s6[:, half], ALU.min)
                nc.sync.dma_start(out_rows[:, u, half], result[:, half])
